import numpy as np
import ml_dtypes


def mxq(x, axis, fmt="e4m3"):
    dtype, down = {"e4m3": (ml_dtypes.float8_e4m3fn, 7), "e5m2": (ml_dtypes.float8_e5m2, 14)}[fmt]
    v = np.moveaxis(np.asarray(x, np.float32).astype(ml_dtypes.bfloat16).astype(np.float64), axis, -1)
    blocks = v.reshape(v.shape[:-1] + (-1, 32))
    amax = np.abs(blocks).max(-1, keepdims=True)
    byte = np.maximum(np.where(amax > 0, np.frexp(amax)[1] - 1 + 127, 0) - down, 1)
    scale = np.exp2(byte - 127.0)
    codes = (blocks / scale).astype(np.float32).astype(dtype).astype(np.float64)
    return np.moveaxis((codes * scale).reshape(v.shape), -1, axis)


WIDE = False


def mx_kscale(k, group=512):
    if not WIDE:
        return np.ones(k)
    levels = np.array([10, -10, 5, -5, 0])
    if group != 512:
        return np.exp2(np.random.permutation(np.resize(levels, k // group))).repeat(group)
    if k % 512:
        return np.exp2(np.random.permutation(np.resize(levels, k // 32))).repeat(32)
    a = np.empty((k // 512, 16))
    for p in range(k // 512):
        a[p, :8] = np.random.permutation(np.resize(levels, 8))
        for g in range(8):
            far = levels[np.abs(levels - a[p, g]) >= 10]
            a[p, g + 8] = far[np.random.randint(len(far))]
    return np.exp2(a.ravel()).repeat(32)


def f64(x):
    return np.asarray(x).astype(np.float64)


def silu(v):
    return v / (1.0 + np.exp(-v))


G, D, M, N = 2, 256, 128, 512


def setup_inputs():
    n = np.random.standard_normal
    s = mx_kscale(D, 0)[:, None]
    return {
        "x": (n((G, D, N)) * s).astype(np.float32),
        "w": (n((G, D, M)) / np.sqrt(D) / s).astype(np.float32),
        "u": (n((G, D, M)) / np.sqrt(D) / s).astype(np.float32),
        "r": n((G, M, N)).astype(np.float32),
    }


def reference(x, w, u, r):
    xq = mxq(f64(x), 1, "e4m3")
    h = mxq(f64(w), 1, "e4m3").transpose(0, 2, 1) @ xq
    g = mxq(f64(u), 1, "e4m3").transpose(0, 2, 1) @ xq
    y = silu(h) * g
    y = y + f64(r)
    return y

@@ -1,0 +1,175 @@
+from contextlib import ExitStack
+
+import concourse.mybir as mybir
+
+G, D, M, N = 2, 256, 128, 512
+FLOPS = 2 * 2 * G * D * M * N
+
+F32 = mybir.dt.float32
+BF16 = mybir.dt.bfloat16
+U32 = mybir.dt.uint32
+U8 = mybir.dt.uint8
+FP8X4 = mybir.dt.float8_e4m3fn_x4
+SILU = mybir.ActivationFunctionType.Silu
+ALU = mybir.AluOpType
+
+P = 128
+PACK = 4
+ROWS = D // PACK
+
+CHUNKS = [256,256]
+STARTS = [sum(CHUNKS[:i]) for i in range(len(CHUNKS))]
+NMM = 128
+
+
+def tile_rows_gglu_silu_res_kernel(tc, x, w, u, r, out):
+    nc = tc.nc
+    with ExitStack() as ctx:
+        sb = ctx.enter_context(tc.tile_pool(name="sb", bufs=1))
+        ps = ctx.enter_context(tc.psum_pool(name="ps", bufs=1))
+        xv = x.rearrange("g (p j) n -> (g p) j n", j=PACK)
+        wv = w.rearrange("g (p j) m -> (g p) j m", j=PACK)
+        uv = u.rearrange("g (p j) m -> (g p) j m", j=PACK)
+        rv = r.rearrange("g m n -> m g n")
+        ov = out.rearrange("g m n -> m g n")
+        nch = len(CHUNKS)
+        x_raw = [sb.tile([P, PACK, CHUNKS[c]], F32, name="xraw%d" % c, align_bytes=64) for c in range(nch)]
+        x_bf = [sb.tile([P, CHUNKS[c], PACK], BF16, name="xbf%d" % c, align_bytes=64) for c in range(nch)]
+        x_codes = sb.tile([P, N], U32, name="xcodes", align_bytes=64)
+        x_scales = sb.tile([P, N], U8, name="xscales", align_bytes=64)
+        wu_raw = [sb.tile([P, PACK, M], F32, name="wuraw%d" % i, align_bytes=64) for i in range(2)]
+        wu_bf = sb.tile([P, 2 * M, PACK], BF16, name="wubf", align_bytes=64)
+        wu_codes = sb.tile([P, 2 * M], U32, name="wucodes", align_bytes=64)
+        wu_scales = sb.tile([P, 2 * M], U8, name="wuscales", align_bytes=64)
+        warm = sb.tile([P, 8], F32, name="warm")
+        warm2 = sb.tile([P, 8], F32, name="warm2")
+        r_sb = sb.tile([P, G, N], F32, name="rsb", align_bytes=64)
+        act = sb.tile([P, G, N], F32, name="act", align_bytes=64)
+        prod = sb.tile([P, G, N], F32, name="prod", align_bytes=64)
+        res = sb.tile([P, G, N], F32, name="res", align_bytes=64)
+        banks = {}
+
+        def bank(key):
+            if key not in banks:
+                banks[key] = ps.tile([P, 512], F32, name="bank_%d_%d_%d" % key)
+            return banks[key]
+
+        def load_x(c, q=nc.sync):
+            q.dma_start(out=x_raw[c][:], in_=xv[:, :, STARTS[c] : STARTS[c] + CHUNKS[c]])
+
+        def load_wu(i, q=nc.sync):
+            q.dma_start(out=wu_raw[i][:], in_=(wv, uv)[i])
+
+        def load_r(a, b, q=nc.sync):
+            q.dma_start(out=r_sb[:, :, a:b], in_=rv[:, :, a:b])
+
+        def load_rg(g, q=nc.sync):
+            q.dma_start(out=r_sb[:, g, :], in_=rv[:, g, :])
+
+        def inter(eng, dst, src):
+            d = dst.rearrange("p (c i) t -> p c t i", i=4)
+            s = src.rearrange("p t (c i) -> p c t i", i=4)
+            if eng == "v":
+                nc.vector.tensor_copy(out=d, in_=s)
+            else:
+                nc.scalar.copy(out=d, in_=s)
+
+        def copy_x(eng, c, a, b):
+            inter(eng, x_bf[c][:, a:b, :], x_raw[c][:, :, a:b])
+
+        def copy_wu(eng, i, a=0, b=M):
+            inter(eng, wu_bf[:, i * M + a : i * M + b, :], wu_raw[i][:, :, a:b])
+
+        def quant_x(c, a=0, b=None):
+            b = CHUNKS[c] if b is None else b
+            cols = slice(STARTS[c] + a, STARTS[c] + b)
+            nc.vector.quantize_mx(
+                out=x_codes[:, cols].bitcast(FP8X4),
+                scales=x_scales[:, cols],
+                in_=x_bf[c][:, a:b, :].rearrange("p n t -> p (n t)"),
+            )
+
+        def quant_wu(a, b):
+            nc.vector.quantize_mx(
+                out=wu_codes[:, a:b].bitcast(FP8X4),
+                scales=wu_scales[:, a:b],
+                in_=wu_bf[:, a:b, :].rearrange("p n t -> p (n t)"),
+            )
+
+        def acc(i, g, a, b):
+            key, off = where(i, g, a)
+            return bank(key)[:, off : off + (b - a)]
+
+        def mm(i, g, a, b):
+            rows = slice(g * ROWS, (g + 1) * ROWS)
+            for n0 in range(a, b, NMM):
+                nc.tensor.matmul_mx(
+                    out=acc(i, g, n0, n0 + NMM),
+                    lhsT=wu_codes[rows, i * M : (i + 1) * M].bitcast(FP8X4),
+                    lhsT_scale=wu_scales[rows, i * M : (i + 1) * M],
+                    rhs=x_codes[rows, n0 : n0 + NMM].bitcast(FP8X4),
+                    rhs_scale=x_scales[rows, n0 : n0 + NMM],
+                    start=True,
+                    stop=True,
+                )
+
+        def silu(g, a, b):
+            nc.scalar.activation(out=act[:, g, a:b], in_=acc(0, g, a, b), func=SILU)
+
+        def mul(g, a, b):
+            nc.vector.tensor_tensor(out=prod[:, g, a:b], in0=acc(1, g, a, b), in1=act[:, g, a:b], op=ALU.mult)
+
+        def add(gs, a, b, eng=nc.vector):
+            eng.tensor_tensor(out=res[:, gs, a:b], in0=prod[:, gs, a:b], in1=r_sb[:, gs, a:b], op=ALU.add)
+
+        def store(gs, a, b, q=nc.sync):
+            q.dma_start(out=ov[:, gs, a:b], in_=res[:, gs, a:b])
+
+        def warmup():
+            nc.gpsimd.memset(warm[:], 0.0)
+            nc.scalar.activation(out=warm2[:], in_=warm[:], func=SILU)
+
+        both = slice(0, 2)
+        ctx.enter_context(tc.manual_schedule())
+
+        def where(i, g, a):
+            return (i, g, a // 256), a % 256
+
+        warmup()
+        load_x(0)
+        load_wu(0)
+        load_wu(1)
+        load_x(1)
+        load_r(0, 256)
+        load_r(256, 512)
+        copy_x("v", 0, 0, 256)
+        copy_wu("s", 0)
+        quant_x(0)
+        copy_wu("s", 1)
+        quant_wu(0, 128)
+        mm(0, 0, 0, 256)
+        mm(0, 1, 0, 256)
+        quant_wu(128, 256)
+        mm(1, 0, 0, 256)
+        mm(1, 1, 0, 256)
+        silu(0, 0, 256)
+        copy_x("v", 1, 0, 160)
+        copy_x("s", 1, 160, 256)
+        silu(1, 0, 256)
+        mul(0, 0, 256)
+        quant_x(1)
+        mm(0, 0, 256, 512)
+        mm(0, 1, 256, 512)
+        mm(1, 0, 256, 512)
+        mm(1, 1, 256, 512)
+        mul(1, 0, 256)
+        add(both, 0, 256)
+        store(both, 0, 256)
+        silu(0, 256, 512)
+        silu(1, 256, 512)
+        mul(0, 256, 512)
+        mul(1, 256, 512)
+        add(0, 256, 512)
+        store(0, 256, 512)
+        add(1, 256, 512)
+        store(1, 256, 512, nc.scalar)

@@ -17,7 +17,7 @@ P = 128
 PACK = 4
 ROWS = D // PACK
 
-CHUNKS = [256,256]
+CHUNKS = [128,128,128,128]
 STARTS = [sum(CHUNKS[:i]) for i in range(len(CHUNKS))]
 NMM = 128
 
@@ -133,42 +133,62 @@ def tile_rows_gglu_silu_res_kernel(tc, x, w, u, r, out):
         ctx.enter_context(tc.manual_schedule())
 
         def where(i, g, a):
-            return (i, g, a // 256), a % 256
+            return (i, g, (a // 128) % 2), (a // 256) * 128
 
-        warmup()
+        def mms(i, c):
+            for g in range(2):
+                mm(i, g, 128 * c, 128 * c + 128)
+
+        def silus(c):
+            for g in range(2):
+                silu(g, 128 * c, 128 * c + 128)
+
+        def muls(c):
+            for g in range(2):
+                mul(g, 128 * c, 128 * c + 128)
+
+
         load_x(0)
         load_wu(0)
         load_wu(1)
         load_x(1)
+        load_x(2)
+        load_x(3)
         load_r(0, 256)
         load_r(256, 512)
-        copy_x("v", 0, 0, 256)
-        copy_wu("s", 0)
+        copy_x("v", 0, 0, 128)
+        copy_wu("v", 0, 0, 128)
         quant_x(0)
-        copy_wu("s", 1)
         quant_wu(0, 128)
-        mm(0, 0, 0, 256)
-        mm(0, 1, 0, 256)
+        mms(0, 0)
+        copy_wu("v", 1, 0, 128)
+        copy_x("v", 1, 0, 128)
         quant_wu(128, 256)
-        mm(1, 0, 0, 256)
-        mm(1, 1, 0, 256)
-        silu(0, 0, 256)
-        copy_x("v", 1, 0, 160)
-        copy_x("s", 1, 160, 256)
-        silu(1, 0, 256)
-        mul(0, 0, 256)
+        mms(1, 0)
         quant_x(1)
-        mm(0, 0, 256, 512)
-        mm(0, 1, 256, 512)
-        mm(1, 0, 256, 512)
-        mm(1, 1, 256, 512)
-        mul(1, 0, 256)
-        add(both, 0, 256)
+        silus(0)
+        mms(0, 1)
+        mms(1, 1)
+        copy_x("s", 2, 96, 128)
+        copy_x("v", 2, 0, 96)
+        copy_x("s", 3, 32, 128)
+        copy_x("v", 3, 0, 32)
+        quant_x(2)
+        mms(0, 2)
+        muls(0)
+        mms(1, 2)
+        silus(1)
+        quant_x(3)
+        mms(0, 3)
+        silus(2)
+        muls(1)
+        mms(1, 3)
+        silus(3)
+        add(both, 0, 128)
+        muls(2)
+        add(both, 128, 256)
         store(both, 0, 256)
-        silu(0, 256, 512)
-        silu(1, 256, 512)
-        mul(0, 256, 512)
-        mul(1, 256, 512)
+        muls(3)
         add(0, 256, 512)
         store(0, 256, 512)
         add(1, 256, 512)

@@ -16,10 +16,12 @@ ALU = mybir.AluOpType
 P = 128
 PACK = 4
 ROWS = D // PACK
-
-CHUNKS = [128,128,128,128]
-STARTS = [sum(CHUNKS[:i]) for i in range(len(CHUNKS))]
-NMM = 128
+CHUNK = 128
+CHUNKS = N // CHUNK
+BANK = 512
+RUN = 4
+W, U = 0, 1
+LAST_ON_VECTOR = 48
 
 
 def tile_rows_gglu_silu_res_kernel(tc, x, w, u, r, out):
@@ -27,169 +29,137 @@ def tile_rows_gglu_silu_res_kernel(tc, x, w, u, r, out):
     with ExitStack() as ctx:
         sb = ctx.enter_context(tc.tile_pool(name="sb", bufs=1))
         ps = ctx.enter_context(tc.psum_pool(name="ps", bufs=1))
-        xv = x.rearrange("g (p j) n -> (g p) j n", j=PACK)
-        wv = w.rearrange("g (p j) m -> (g p) j m", j=PACK)
-        uv = u.rearrange("g (p j) m -> (g p) j m", j=PACK)
-        rv = r.rearrange("g m n -> m g n")
-        ov = out.rearrange("g m n -> m g n")
-        nch = len(CHUNKS)
-        x_raw = [sb.tile([P, PACK, CHUNKS[c]], F32, name="xraw%d" % c, align_bytes=64) for c in range(nch)]
-        x_bf = [sb.tile([P, CHUNKS[c], PACK], BF16, name="xbf%d" % c, align_bytes=64) for c in range(nch)]
-        x_codes = sb.tile([P, N], U32, name="xcodes", align_bytes=64)
-        x_scales = sb.tile([P, N], U8, name="xscales", align_bytes=64)
-        wu_raw = [sb.tile([P, PACK, M], F32, name="wuraw%d" % i, align_bytes=64) for i in range(2)]
-        wu_bf = sb.tile([P, 2 * M, PACK], BF16, name="wubf", align_bytes=64)
-        wu_codes = sb.tile([P, 2 * M], U32, name="wucodes", align_bytes=64)
-        wu_scales = sb.tile([P, 2 * M], U8, name="wuscales", align_bytes=64)
-        warm = sb.tile([P, 8], F32, name="warm")
-        warm2 = sb.tile([P, 8], F32, name="warm2")
-        r_sb = sb.tile([P, G, N], F32, name="rsb", align_bytes=64)
-        act = sb.tile([P, G, N], F32, name="act", align_bytes=64)
-        prod = sb.tile([P, G, N], F32, name="prod", align_bytes=64)
-        res = sb.tile([P, G, N], F32, name="res", align_bytes=64)
+
+        x_hbm = x.rearrange("g (p j) n -> (g p) j n", j=PACK)
+        weights_hbm = [t.rearrange("g (p j) m -> (g p) j m", j=PACK) for t in (w, u)]
+        r_hbm = r.rearrange("g m n -> m g n")
+        out_hbm = out.rearrange("g m n -> m g n")
+
+        x_raw = [sb.tile([P, PACK, CHUNK], F32, name="x_raw%d" % c, align_bytes=64) for c in range(CHUNKS)]
+        x_bf = [sb.tile([P, CHUNK, PACK], BF16, name="x_bf%d" % c, align_bytes=64) for c in range(CHUNKS)]
+        x_codes = sb.tile([P, N], U32, name="x_codes", align_bytes=64)
+        x_scales = sb.tile([P, N], U8, name="x_scales", align_bytes=64)
+        weights_raw = [sb.tile([P, PACK, M], F32, name="weights_raw%d" % i, align_bytes=64) for i in (W, U)]
+        weights_bf = sb.tile([P, 2 * M, PACK], BF16, name="weights_bf", align_bytes=64)
+        weights_codes = sb.tile([P, 2 * M], U32, name="weights_codes", align_bytes=64)
+        weights_scales = sb.tile([P, 2 * M], U8, name="weights_scales", align_bytes=64)
+        r_sb = sb.tile([P, G, N], F32, name="r_sb", align_bytes=64)
+        activated = sb.tile([P, G, N], F32, name="activated", align_bytes=64)
+        gated = sb.tile([P, G, N], F32, name="gated", align_bytes=64)
+        result = sb.tile([P, G, N], F32, name="result", align_bytes=64)
         banks = {}
+        for parity in range(2):
+            for i in (W, U):
+                for g in range(G):
+                    banks[i, g, parity] = ps.tile([P, BANK], F32, name="bank_%d_%d_%d" % (i, g, parity))
 
-        def bank(key):
-            if key not in banks:
-                banks[key] = ps.tile([P, 512], F32, name="bank_%d_%d_%d" % key)
-            return banks[key]
+        def cols(c):
+            return slice(c * CHUNK, (c + 1) * CHUNK)
 
-        def load_x(c, q=nc.sync):
-            q.dma_start(out=x_raw[c][:], in_=xv[:, :, STARTS[c] : STARTS[c] + CHUNKS[c]])
+        def weight_cols(i):
+            return slice(i * M, (i + 1) * M)
 
-        def load_wu(i, q=nc.sync):
-            q.dma_start(out=wu_raw[i][:], in_=(wv, uv)[i])
+        def sums(i, g, c):
+            return banks[i, g, c % 2][:, cols(c // 2)]
 
-        def load_r(a, b, q=nc.sync):
-            q.dma_start(out=r_sb[:, :, a:b], in_=rv[:, :, a:b])
+        def load_x(c):
+            nc.sync.dma_start(out=x_raw[c][:], in_=x_hbm[:, :, cols(c)])
 
-        def load_rg(g, q=nc.sync):
-            q.dma_start(out=r_sb[:, g, :], in_=rv[:, g, :])
-
-        def inter(eng, dst, src):
-            d = dst.rearrange("p (c i) t -> p c t i", i=4)
-            s = src.rearrange("p t (c i) -> p c t i", i=4)
-            if eng == "v":
-                nc.vector.tensor_copy(out=d, in_=s)
-            else:
-                nc.scalar.copy(out=d, in_=s)
-
-        def copy_x(eng, c, a, b):
-            inter(eng, x_bf[c][:, a:b, :], x_raw[c][:, :, a:b])
-
-        def copy_wu(eng, i, a=0, b=M):
-            inter(eng, wu_bf[:, i * M + a : i * M + b, :], wu_raw[i][:, :, a:b])
-
-        def quant_x(c, a=0, b=None):
-            b = CHUNKS[c] if b is None else b
-            cols = slice(STARTS[c] + a, STARTS[c] + b)
-            nc.vector.quantize_mx(
-                out=x_codes[:, cols].bitcast(FP8X4),
-                scales=x_scales[:, cols],
-                in_=x_bf[c][:, a:b, :].rearrange("p n t -> p (n t)"),
+        def interleave(copy, bf, raw):
+            copy(
+                out=bf.rearrange("p (c i) j -> p c j i", i=RUN),
+                in_=raw.rearrange("p j (c i) -> p c j i", i=RUN),
             )
 
-        def quant_wu(a, b):
-            nc.vector.quantize_mx(
-                out=wu_codes[:, a:b].bitcast(FP8X4),
-                scales=wu_scales[:, a:b],
-                in_=wu_bf[:, a:b, :].rearrange("p n t -> p (n t)"),
-            )
+        def interleave_x(c, copy=nc.vector.tensor_copy, part=slice(0, CHUNK)):
+            interleave(copy, x_bf[c][:, part, :], x_raw[c][:, :, part])
 
-        def acc(i, g, a, b):
-            key, off = where(i, g, a)
-            return bank(key)[:, off : off + (b - a)]
+        def interleave_weights(i):
+            interleave(nc.vector.tensor_copy, weights_bf[:, weight_cols(i), :], weights_raw[i][:])
 
-        def mm(i, g, a, b):
-            rows = slice(g * ROWS, (g + 1) * ROWS)
-            for n0 in range(a, b, NMM):
+        def quantize(codes, scales, bf):
+            nc.vector.quantize_mx(out=codes.bitcast(FP8X4), scales=scales, in_=bf.rearrange("p n j -> p (n j)"))
+
+        def quantize_x(c):
+            quantize(x_codes[:, cols(c)], x_scales[:, cols(c)], x_bf[c][:])
+
+        def quantize_weights(i):
+            k = weight_cols(i)
+            quantize(weights_codes[:, k], weights_scales[:, k], weights_bf[:, k, :])
+
+        def matmuls(i, c):
+            for g in range(G):
+                rows = slice(g * ROWS, (g + 1) * ROWS)
                 nc.tensor.matmul_mx(
-                    out=acc(i, g, n0, n0 + NMM),
-                    lhsT=wu_codes[rows, i * M : (i + 1) * M].bitcast(FP8X4),
-                    lhsT_scale=wu_scales[rows, i * M : (i + 1) * M],
-                    rhs=x_codes[rows, n0 : n0 + NMM].bitcast(FP8X4),
-                    rhs_scale=x_scales[rows, n0 : n0 + NMM],
+                    out=sums(i, g, c),
+                    lhsT=weights_codes[rows, weight_cols(i)].bitcast(FP8X4),
+                    lhsT_scale=weights_scales[rows, weight_cols(i)],
+                    rhs=x_codes[rows, cols(c)].bitcast(FP8X4),
+                    rhs_scale=x_scales[rows, cols(c)],
                     start=True,
                     stop=True,
                 )
 
-        def silu(g, a, b):
-            nc.scalar.activation(out=act[:, g, a:b], in_=acc(0, g, a, b), func=SILU)
+        def silu(c):
+            for g in range(G):
+                nc.scalar.activation(out=activated[:, g, cols(c)], in_=sums(W, g, c), func=SILU)
 
-        def mul(g, a, b):
-            nc.vector.tensor_tensor(out=prod[:, g, a:b], in0=acc(1, g, a, b), in1=act[:, g, a:b], op=ALU.mult)
+        def gate(c):
+            for g in range(G):
+                nc.vector.tensor_tensor(
+                    out=gated[:, g, cols(c)], in0=sums(U, g, c), in1=activated[:, g, cols(c)], op=ALU.mult
+                )
 
-        def add(gs, a, b, eng=nc.vector):
-            eng.tensor_tensor(out=res[:, gs, a:b], in0=prod[:, gs, a:b], in1=r_sb[:, gs, a:b], op=ALU.add)
+        def add_and_store(c, groups=slice(0, G), queue=nc.sync):
+            nc.vector.tensor_tensor(
+                out=result[:, groups, cols(c)], in0=gated[:, groups, cols(c)], in1=r_sb[:, groups, cols(c)], op=ALU.add
+            )
+            queue.dma_start(out=out_hbm[:, groups, cols(c)], in_=result[:, groups, cols(c)])
 
-        def store(gs, a, b, q=nc.sync):
-            q.dma_start(out=ov[:, gs, a:b], in_=res[:, gs, a:b])
-
-        def warmup():
-            nc.gpsimd.memset(warm[:], 0.0)
-            nc.scalar.activation(out=warm2[:], in_=warm[:], func=SILU)
-
-        both = slice(0, 2)
         ctx.enter_context(tc.manual_schedule())
 
-        def where(i, g, a):
-            return (i, g, (a // 128) % 2), (a // 256) * 128
-
-        def mms(i, c):
-            for g in range(2):
-                mm(i, g, 128 * c, 128 * c + 128)
-
-        def silus(c):
-            for g in range(2):
-                silu(g, 128 * c, 128 * c + 128)
-
-        def muls(c):
-            for g in range(2):
-                mul(g, 128 * c, 128 * c + 128)
-
-
         load_x(0)
-        load_wu(0)
-        load_wu(1)
-        load_x(1)
-        load_x(2)
-        load_x(3)
-        load_r(0, 256)
-        load_r(256, 512)
-        copy_x("v", 0, 0, 128)
-        copy_wu("v", 0, 0, 128)
-        quant_x(0)
-        quant_wu(0, 128)
-        mms(0, 0)
-        copy_wu("v", 1, 0, 128)
-        copy_x("v", 1, 0, 128)
-        quant_wu(128, 256)
-        mms(1, 0)
-        quant_x(1)
-        silus(0)
-        mms(0, 1)
-        mms(1, 1)
-        copy_x("s", 2, 96, 128)
-        copy_x("v", 2, 0, 96)
-        copy_x("s", 3, 32, 128)
-        copy_x("v", 3, 0, 32)
-        quant_x(2)
-        mms(0, 2)
-        muls(0)
-        mms(1, 2)
-        silus(1)
-        quant_x(3)
-        mms(0, 3)
-        silus(2)
-        muls(1)
-        mms(1, 3)
-        silus(3)
-        add(both, 0, 128)
-        muls(2)
-        add(both, 128, 256)
-        store(both, 0, 256)
-        muls(3)
-        add(0, 256, 512)
-        store(0, 256, 512)
-        add(1, 256, 512)
-        store(1, 256, 512, nc.scalar)
+        for i in (W, U):
+            nc.sync.dma_start(out=weights_raw[i][:], in_=weights_hbm[i])
+        for c in range(1, CHUNKS):
+            load_x(c)
+        for half in (slice(0, N // 2), slice(N // 2, N)):
+            nc.sync.dma_start(out=r_sb[:, :, half], in_=r_hbm[:, :, half])
+
+        interleave_x(0)
+        interleave_weights(W)
+        quantize_x(0)
+        quantize_weights(W)
+        matmuls(W, 0)
+
+        interleave_weights(U)
+        interleave_x(1)
+        quantize_weights(U)
+        matmuls(U, 0)
+        quantize_x(1)
+        silu(0)
+        matmuls(W, 1)
+        matmuls(U, 1)
+
+        interleave_x(2)
+        interleave_x(3, nc.scalar.copy, slice(LAST_ON_VECTOR, CHUNK))
+        interleave_x(3, part=slice(0, LAST_ON_VECTOR))
+        quantize_x(2)
+
+        matmuls(W, 2)
+        gate(0)
+        matmuls(U, 2)
+        silu(1)
+        quantize_x(3)
+        matmuls(W, 3)
+        silu(2)
+        gate(1)
+        matmuls(U, 3)
+        silu(3)
+
+        for c in range(CHUNKS - 1):
+            add_and_store(c)
+            if c + 2 < CHUNKS:
+                gate(c + 2)
+        add_and_store(CHUNKS - 1, 0)
+        add_and_store(CHUNKS - 1, 1, nc.scalar)

from contextlib import ExitStack

import concourse.mybir as mybir

G, D, M, N = 2, 256, 128, 512
FLOPS = 2 * 2 * G * D * M * N

F32 = mybir.dt.float32
BF16 = mybir.dt.bfloat16
U32 = mybir.dt.uint32
U8 = mybir.dt.uint8
FP8X4 = mybir.dt.float8_e4m3fn_x4
SILU = mybir.ActivationFunctionType.Silu
ALU = mybir.AluOpType

P = 128
PACK = 4
ROWS = D // PACK
CHUNK = 128
CHUNKS = N // CHUNK
BANK = 512
RUN = 4
W, U = 0, 1
LAST_ON_VECTOR = 48


def tile_rows_gglu_silu_res_kernel(tc, x, w, u, r, out):
    nc = tc.nc
    with ExitStack() as ctx:
        sb = ctx.enter_context(tc.tile_pool(name="sb", bufs=1))
        ps = ctx.enter_context(tc.psum_pool(name="ps", bufs=1))

        x_hbm = x.rearrange("g (p j) n -> (g p) j n", j=PACK)
        weights_hbm = [t.rearrange("g (p j) m -> (g p) j m", j=PACK) for t in (w, u)]
        r_hbm = r.rearrange("g m n -> m g n")
        out_hbm = out.rearrange("g m n -> m g n")

        x_raw = [sb.tile([P, PACK, CHUNK], F32, name="x_raw%d" % c, align_bytes=64) for c in range(CHUNKS)]
        x_bf = [sb.tile([P, CHUNK, PACK], BF16, name="x_bf%d" % c, align_bytes=64) for c in range(CHUNKS)]
        x_codes = sb.tile([P, N], U32, name="x_codes", align_bytes=64)
        x_scales = sb.tile([P, N], U8, name="x_scales", align_bytes=64)
        weights_raw = [sb.tile([P, PACK, M], F32, name="weights_raw%d" % i, align_bytes=64) for i in (W, U)]
        weights_bf = sb.tile([P, 2 * M, PACK], BF16, name="weights_bf", align_bytes=64)
        weights_codes = sb.tile([P, 2 * M], U32, name="weights_codes", align_bytes=64)
        weights_scales = sb.tile([P, 2 * M], U8, name="weights_scales", align_bytes=64)
        r_sb = sb.tile([P, G, N], F32, name="r_sb", align_bytes=64)
        activated = sb.tile([P, G, N], F32, name="activated", align_bytes=64)
        gated = sb.tile([P, G, N], F32, name="gated", align_bytes=64)
        result = sb.tile([P, G, N], F32, name="result", align_bytes=64)
        banks = {}
        for parity in range(2):
            for i in (W, U):
                for g in range(G):
                    banks[i, g, parity] = ps.tile([P, BANK], F32, name="bank_%d_%d_%d" % (i, g, parity))

        def cols(c):
            return slice(c * CHUNK, (c + 1) * CHUNK)

        def weight_cols(i):
            return slice(i * M, (i + 1) * M)

        def sums(i, g, c):
            return banks[i, g, c % 2][:, cols(c // 2)]

        def load_x(c):
            nc.sync.dma_start(out=x_raw[c][:], in_=x_hbm[:, :, cols(c)])

        def interleave(copy, bf, raw):
            copy(
                out=bf.rearrange("p (c i) j -> p c j i", i=RUN),
                in_=raw.rearrange("p j (c i) -> p c j i", i=RUN),
            )

        def interleave_x(c, copy=nc.vector.tensor_copy, part=slice(0, CHUNK)):
            interleave(copy, x_bf[c][:, part, :], x_raw[c][:, :, part])

        def interleave_weights(i):
            interleave(nc.vector.tensor_copy, weights_bf[:, weight_cols(i), :], weights_raw[i][:])

        def quantize(codes, scales, bf):
            nc.vector.quantize_mx(out=codes.bitcast(FP8X4), scales=scales, in_=bf.rearrange("p n j -> p (n j)"))

        def quantize_x(c):
            quantize(x_codes[:, cols(c)], x_scales[:, cols(c)], x_bf[c][:])

        def quantize_weights(i):
            k = weight_cols(i)
            quantize(weights_codes[:, k], weights_scales[:, k], weights_bf[:, k, :])

        def matmuls(i, c):
            for g in range(G):
                rows = slice(g * ROWS, (g + 1) * ROWS)
                nc.tensor.matmul_mx(
                    out=sums(i, g, c),
                    lhsT=weights_codes[rows, weight_cols(i)].bitcast(FP8X4),
                    lhsT_scale=weights_scales[rows, weight_cols(i)],
                    rhs=x_codes[rows, cols(c)].bitcast(FP8X4),
                    rhs_scale=x_scales[rows, cols(c)],
                    start=True,
                    stop=True,
                )

        def silu(c):
            for g in range(G):
                nc.scalar.activation(out=activated[:, g, cols(c)], in_=sums(W, g, c), func=SILU)

        def gate(c):
            for g in range(G):
                nc.vector.tensor_tensor(
                    out=gated[:, g, cols(c)], in0=sums(U, g, c), in1=activated[:, g, cols(c)], op=ALU.mult
                )

        def add_and_store(c, groups=slice(0, G), queue=nc.sync):
            nc.vector.tensor_tensor(
                out=result[:, groups, cols(c)], in0=gated[:, groups, cols(c)], in1=r_sb[:, groups, cols(c)], op=ALU.add
            )
            queue.dma_start(out=out_hbm[:, groups, cols(c)], in_=result[:, groups, cols(c)])

        ctx.enter_context(tc.manual_schedule())

        load_x(0)
        for i in (W, U):
            nc.sync.dma_start(out=weights_raw[i][:], in_=weights_hbm[i])
        for c in range(1, CHUNKS):
            load_x(c)
        for half in (slice(0, N // 2), slice(N // 2, N)):
            nc.sync.dma_start(out=r_sb[:, :, half], in_=r_hbm[:, :, half])

        interleave_x(0)
        interleave_weights(W)
        quantize_x(0)
        quantize_weights(W)
        matmuls(W, 0)

        interleave_weights(U)
        interleave_x(1)
        quantize_weights(U)
        matmuls(U, 0)
        quantize_x(1)
        silu(0)
        matmuls(W, 1)
        matmuls(U, 1)

        interleave_x(2)
        interleave_x(3, nc.scalar.copy, slice(LAST_ON_VECTOR, CHUNK))
        interleave_x(3, part=slice(0, LAST_ON_VECTOR))
        quantize_x(2)

        matmuls(W, 2)
        gate(0)
        matmuls(U, 2)
        silu(1)
        quantize_x(3)
        matmuls(W, 3)
        silu(2)
        gate(1)
        matmuls(U, 3)
        silu(3)

        for c in range(CHUNKS - 1):
            add_and_store(c)
            if c + 2 < CHUNKS:
                gate(c + 2)
        add_and_store(CHUNKS - 1, 0)
        add_and_store(CHUNKS - 1, 1, nc.scalar)
